import numpy as np, ml_dtypes
CORES = [2,6,10,14,18,22,26,30]
N = 8
BF = ml_dtypes.bfloat16
def gentries(a):
    return np.ascontiguousarray(a.reshape(8, 16, -1).transpose(0, 2, 1)).reshape(8, -1)
def gtable(e):
    e = np.asarray(e); return np.ascontiguousarray(e.reshape(8, -1, 16).transpose(0, 2, 1)).reshape(128, -1).astype(np.int32)
V, G, B, L, RO = 2048, 128, 3, 128, 2
W = V + B * G
def numbers(rng, ghost):
    s = (N, 8, V, 16)
    return np.where(rng.random(s) < ghost, rng.integers(V, W, s), rng.integers(0, V, s))
def image(t, nb):
    tw = np.concatenate([t, np.broadcast_to(np.arange(V, W), (N, 8, W - V))], axis=2)
    e = np.take_along_axis(tw, nb.reshape(N, 8, -1), 2).reshape(nb.shape)
    return np.take_along_axis(e, np.argsort(t, axis=-1)[..., None], 2)
def parts(rng, z, wild, mix):
    t = np.argsort(rng.random((N, 8, V)), axis=-1); nb = numbers(rng, 0.125)
    nz = np.where(rng.random(nb.shape) < wild, numbers(rng, 0.125), image(t, nb))
    x = np.clip(np.take_along_axis(z, t[:, :, None, :], 3) + rng.integers(-2, 3, z.shape), 0, 255)
    x = np.where(rng.random(z.shape) < 0.1, rng.integers(0, 256, z.shape), x)
    o = np.argsort(rng.random((N, 8, V)), axis=-1); m = t.copy()
    for r in range(N):
        for g in range(8):
            j = o[r, g, :int(V * mix[r, g])]; m[r, g, j] = t[r, g, np.roll(j, 1)]
    bx = np.ascontiguousarray(np.argsort(rng.random((N, 8, V)), axis=-1)[..., :G]); bz = np.take_along_axis(t, bx, 2)
    return {"x": x, "z": z, "nb": nb, "nz": nz, "m": m, "bx": bx, "bz": bz}
def pack(d):
    return {"x": np.ascontiguousarray(d["x"].reshape(N, 128, V)).astype(np.float32).astype(BF), "z": np.ascontiguousarray(d["z"].reshape(N, 128, V)).astype(np.float32).astype(BF),
            "nb": np.stack([gtable(a.reshape(8, -1)) for a in d["nb"]]), "nz": np.stack([gtable(a.reshape(8, -1)) for a in d["nz"]]),
            "m": d["m"].astype(np.int32), "im": np.argsort(d["m"], axis=-1).astype(np.int32),
            "bx": np.stack([gtable(a) for a in d["bx"]]), "bz": np.stack([gtable(a) for a in d["bz"]])}
def setup_inputs(rng):
    size = rng.permuted(np.tile(np.array([1, 1, 3, 3, 15, 63, 255, 255]), (N, 1)), axis=1)[:, :, None, None]
    z = rng.integers(0, size + 1, (N, 8, 16, V))
    wild = rng.choice(np.array([0.05, 0.2, 0.5, 1.0]), (N, 8, 1, 1)); mix = rng.choice(np.array([0.1, 0.3, 0.6, 1.0]), (N, 8))
    h = int(rng.integers(0, 8)); wild[:, h] = 0.0; mix[:, h] = 0.05
    return pack(parts(rng, z, wild, mix))
def setup_inputs_ties(rng):
    z = rng.integers(0, 2, (N, 8, 16, V)) * (rng.random((N, 8, 1, V)) < 0.5); z[:, 1, 1:] = 0
    d = parts(rng, z, rng.choice(np.array([0.2, 1.0]), (N, 8, 1, 1)), np.full((N, 8), 0.8))
    u = (np.arange(L) * (V // L))[1::2]
    for r in range(N):
        for g in (0, 2, 4, 6):
            s0 = np.flatnonzero(np.all(z[r, g] == 0, axis=0)); im = np.argsort(d["m"][r, g])
            d["nb"][r, g, u] = im[rng.choice(s0, (len(u), 16))]; d["nz"][r, g, d["m"][r, g, u]] = rng.choice(s0, (len(u), 16))
    d["nb"][:, 5] = rng.integers(0, V, (N, 1, 16))
    return pack(d)
def setup_inputs_crowd(rng):
    z = rng.integers(0, rng.choice(np.array([3, 15, 255]), (N, 8, 1, 1)) + 1, (N, 8, 16, V))
    d = parts(rng, z, np.ones((N, 8, 1, 1)), np.ones((N, 8)))
    for r in range(N):
        for g in range(8):
            n = (24, 160)[g % 2]
            s = np.concatenate([np.array([0, V - 1]), 1 + rng.permutation(V - 2)[:n - 2]]); e = np.concatenate([np.array([0, V - 1]), 1 + rng.permutation(V - 2)[:n - 2]])
            if g < 4: e = d["m"][r, g, s]
            ends = np.array([V, W - 1])
            d["nb"][r, g] = np.where(rng.random((V, 16)) < 0.05, rng.choice(ends, (V, 16)), rng.choice(s, (V, 16)))
            d["nz"][r, g] = np.where(rng.random((V, 16)) < 0.05, rng.choice(ends, (V, 16)), rng.choice(e, (V, 16)))
            d["bx"][r, g] = rng.choice(s, G); d["bz"][r, g] = rng.choice(e, G)
    return pack(d)
def setup_inputs_border(rng):
    z = rng.integers(0, rng.choice(np.array([3, 15, 255]), (N, 8, 1, 1)) + 1, (N, 8, 16, V))
    d = parts(rng, z, np.ones((N, 8, 1, 1)), np.ones((N, 8)))
    for r in range(N):
        for g in range(8):
            s = rng.permutation(V)[:160]; e = d["m"][r, g, s]
            d["nb"][r, g] = np.where(rng.random((V, 16)) < 0.3, rng.integers(V, W, (V, 16)), rng.choice(s, (V, 16)))
            d["nz"][r, g] = np.where(rng.random((V, 16)) < 0.3, rng.integers(V, W, (V, 16)), rng.choice(e, (V, 16)))
            d["bx"][r, g] = rng.choice(s, G); d["bz"][r, g] = rng.choice(e, G)
    d["bx"][:, :, 0] = 0; d["bx"][:, :, G - 1] = V - 1; d["bz"][:, :, 0] = V - 1; d["bz"][:, :, G - 1] = 0
    q = rng.permutation(8); d["nb"][:, q[0]] = rng.integers(V, W, (N, V, 16)); d["nz"][:, q[1]] = rng.integers(V, W, (N, V, 16))
    d["nb"][:, :, 0, :2] = np.array([V, W - 1])
    return pack(d)
def agree(d, r, g):
    t = np.concatenate([d["m"][r, g], np.arange(V, W)]); d["nz"][r, g, t[:V]] = t[d["nb"][r, g]]
def early(rng, d, r, g, n):
    st = np.arange(L) * (V // L); o = rng.permutation(np.setdiff1d(np.arange(V), np.concatenate([st, d["bx"][r, g]])))
    p = o[:2 * n]; a = d["nb"][r, g][st]; a[np.isin(a, p)] = o[2 * n]
    a[rng.permutation(L)[:n], rng.integers(0, 16, n)] = p[:n]; d["nb"][r, g, st] = a
    agree(d, r, g); t = d["m"][r, g].copy(); d["m"][r, g, p] = t[np.roll(p, n)]
def late(rng, d, r, g):
    st = np.arange(L) * (V // L); o = rng.permutation(np.setdiff1d(np.arange(V), np.concatenate([st, d["bx"][r, g], np.array([819, V - 1])])))
    p = o[:6].copy(); s = p[:3]; f = int(o[6]); b = o[7:7 + L].copy(); c = o[7 + L:7 + 2 * L].copy(); rest = o[7 + 2 * L:]
    j = 1 + rng.permutation(L - 1)[:3]; b[j[0]] = 819
    nb = d["nb"][r, g]; nb[np.isin(nb, p)] = f
    nb[p] = rng.choice(rest, (6, 16)); nb[s, rng.integers(0, 16, 3)] = f
    nb[st, 0] = b; nb[b, 0] = c; nb[819, 0] = rng.integers(V, W)
    nb[np.array([b[j[1]], c[j[2]], V - 1]), rng.integers(1, 16, 3)] = s
    agree(d, r, g); t = d["m"][r, g].copy(); z = d["z"][r, g]
    z[:] = rng.integers(0, 200, (16, 1)); z[:, t[s]] += rng.integers(1, 5, (16, 3)); z[int(rng.integers(0, 16)), t[f]] += rng.integers(1, 16)
    d["m"][r, g, p] = t[np.roll(p, 3)]
def setup_inputs_still(rng):
    z = rng.integers(0, 256, (N, 8, 16, V)); d = parts(rng, z, np.zeros((N, 8, 1, 1)), np.zeros((N, 8)))
    q, q2, q3 = [int(i) for i in rng.permutation(N)[:3]]; h, h2 = [int(i) for i in rng.permutation(8)[:2]]; st = np.arange(L) * (V // L)
    room = [L] + [(287 - L + i) // 5 for i in range(5)]
    for r in range(N):
        for g in range(8):
            if r == q or g == h: continue
            if r in (q2, q3):
                if g == h2: late(rng, d, r, g)
                elif r == q3: early(rng, d, r, g, room.pop())
                continue
            c = np.unique(d["nb"][r, g, st]); c = np.setdiff1d(c[c < V], np.concatenate([st, d["bx"][r, g]]))
            p = rng.permutation(c)[:2 * int(rng.integers(1, 4))]
            d["m"][r, g, p] = d["m"][r, g, p.reshape(-1, 2)[:, ::-1].reshape(-1)]
    return pack(d)
def setup_inputs_spread(rng):
    z = (np.exp2(8 * rng.random((N, 8, 1, V))) * rng.random((N, 8, 16, V)) * (rng.random((N, 8, 1, V)) > 0.0625)).astype(np.int64)
    wild = rng.choice(np.array([0.05, 0.3, 1.0]), (N, 8, 1, 1)); mix = rng.choice(np.array([0.2, 0.5, 1.0]), (N, 8))
    for h in rng.permutation(8)[:2]:
        u = rng.integers(0, 4, (N, 16, V)); z[:, h] = np.where(rng.random((N, 1, V)) < 0.5, u, 255 - u); wild[:, h] = 1.0; mix[:, h] = 1.0
    return pack(parts(rng, z, wild, mix))
def check_inputs(d):
    bad = []
    for k in ("x", "z"):
        a = np.asarray(d[k]).astype(np.float32)
        if not np.all((a >= 0) & (a <= 255) & (a == np.floor(a))): bad.append("whole numbers 0 to 255 in " + k)
    for k, hi in (("nb", W - 1), ("nz", W - 1), ("m", V - 1), ("im", V - 1), ("bx", V - 1), ("bz", V - 1)):
        if np.min(d[k]) < 0 or np.max(d[k]) > hi: bad.append("range of " + k)
    if not np.all(np.sort(d["m"], axis=-1) == np.arange(V)): bad.append("m is a bijection")
    elif not np.all(np.argsort(d["m"], axis=-1) == d["im"]): bad.append("im is the inverse of m")
    return bad
def reference(x, z, nb, nz, m, im, bx, bz):
    X = x.astype(np.float32).astype(np.int64).reshape(N, 8, 16, V); Z = z.astype(np.float32).astype(np.int64).reshape(N, 8, 16, V)
    nv = np.stack([gentries(a) for a in nb]).astype(np.int64).reshape(N, 8, V, 16); ns = np.stack([gentries(a) for a in nz]).astype(np.int64).reshape(N, 8, V, 16)
    M = m.astype(np.int64); I = im.astype(np.int64)
    b1 = np.stack([gentries(a) for a in bx]).astype(np.int64); b2 = np.stack([gentries(a) for a in bz]).astype(np.int64)
    lane = np.arange(L); v = np.tile(lane * (V // L), (N, 8, 1)); last = np.zeros(N, np.int64)
    for rnd in range(RO):
        Y = np.take_along_axis(Z, M[:, :, None, :], 3)
        ey = np.take_along_axis(Y, b1[:, :, None, :], 3); ez = np.take_along_axis(Z, b2[:, :, None, :], 3)
        YW = np.concatenate([Y] + [np.roll(ey, -d, axis=0) for d in range(1, B + 1)], axis=3)
        ZW = np.concatenate([Z] + [np.roll(ez, -d, axis=0) for d in range(1, B + 1)], axis=3)
        th = last & 31; last = np.zeros(N, np.int64)
        for r in range(N):
            for g in range(8):
                Yg, Zg, n1, n2, at = YW[r, g], ZW[r, g], nv[r, g], ns[r, g], v[r, g].copy()
                na = n1[at]; nq = n2[M[r, g, at]]
                D = np.add.reduce(np.abs(Yg[:, na] - Zg[:, nq]), axis=0); k = np.argmax(D, axis=1)
                a = na[lane, k]; q = nq[lane, k]; live = (D[lane, k] > 0) & (a < V) & (q < V)
                ac = np.minimum(a, V - 1); qc = np.minimum(q, V - 1); w = I[r, g, qc]; p = M[r, g, ac]
                Aa = Yg[:, n1[ac]]; Aw = Yg[:, n1[w]]; Ba = Zg[:, n2[p]]; Bw = Zg[:, n2[qc]]
                gain = np.add.reduce(np.abs(Aa - Ba) + np.abs(Aw - Bw) - np.abs(Aa - Bw) - np.abs(Aw - Ba), axis=(0, 2))
                prop = live & (gain > th[r])
                first = np.full(V, L); np.minimum.at(first, ac[prop], lane[prop]); np.minimum.at(first, w[prop], lane[prop])
                com = prop & (first[ac] >= lane) & (first[w] >= lane)
                last[r] += np.count_nonzero(com)
                v[r, g] = np.where(com, a, np.where(q < V, w, (5 * at + 1) & (V - 1)))
                a, w, p, q = a[com], w[com], p[com], q[com]
                M[r, g, a] = q; M[r, g, w] = p; I[r, g, q] = a; I[r, g, p] = w
                for vert, site in ((a, q), (w, p)):
                    old = Z[r, g][:, site]; Z[r, g][:, site] = old + np.clip(X[r, g][:, vert] - old, -1, 1)
    return {"mo": M.astype(np.float32), "zo": Z.reshape(N, 128, V).astype(np.float32).astype(BF)}

from concourse.bass import DstId, RemoteDMATransfer
from concourse.mybir import AluOpType as A, AxisListType, ActivationFunctionType as F

N, NV, NW, DUMP = 8, 2048, 2432, 2944
ROUNDS = 2


def _buffers():
    s = {}
    def add(names, cols, ty):
        for n in names.split():
            s[n] = ("sbuf", [128, cols], ty)
    add("Z Y", DUMP, "bfloat16"); add("X", NW, "bfloat16")
    add("mrep imrep", DUMP, "float32"); add("nbt nzt", NW, "int32")
    add("mS mc imc", 128, "int32"); add("bxi bzi bci", 8, "int32"); add("l15i", 16, "int32"); add("ip32 pmi pgi tha thb", 1, "int32")
    add("ipf pm pg dc1 dc2 pm16 thh cn", 1, "float32")
    add("rowI rowG If mSf KEY MX OH ones cK", 128, "float32"); add("rowT diag segm PAQ SC E WPm WPs E2", 256, "float32")
    add("rowc", 40, "float32"); add("RD", 40, "float16"); add("rowGG", 1024, "float32"); add("BOg", 1024, "float16")
    add("Ih BOh mch imch EC", 128, "float16"); add("tri RH", 256, "float16"); add("LT RR", 2048, "float16")
    add("Ib prop8 bi16 bip bim", 128, "bfloat16")
    add("ind ind16 vl nv5 own ea WS bad thr thr2 nc tv", 8, "float32"); add("bad2", 16, "float32"); add("nvi", 8, "int32"); add("LST", 32, "float32")
    add("ML nal nql LA LBp LAp LB", 128, "uint16"); add("BXL BZL bc VU MVL", 8, "uint16"); add("L15", 16, "uint16"); add("UL OF", 32, "uint16")
    add("naf nqf", 128, "float32"); add("ZQ DF AD Bp Bb Ap M1 M2 M3 M4", 2048, "bfloat16"); add("EQ", 4096, "bfloat16")
    add("RP", 512, "float32"); add("XD CL ZQP sb0 sb1", 256, "bfloat16")
    for n in ("st0", "st1"):
        s[n] = ("sbuf", [128, 3, 256], "bfloat16")
    for n in range(8):
        s["k%d" % n] = ("psum", [128, 512], "float32")
    return s


SCRATCH = _buffers()
SEMAPHORES = ["qV", "qS", "qP", "qG", "sent", "arr0", "arr1", "dms", "dz", "dmc", "dim", "dbx", "dbz", "dnz", "dnb", "dx", "dzo", "dmo"]


def rank_program(g, core, T, topo):
    rank = T.rank_of(core)
    if rank is None:
        return
    eng = {"V": g.vector, "S": g.scalar, "P": g.tensor, "G": g, "Y": g.sync}
    due = {n: 0 for n in SEMAPHORES}
    know = {q: {} for q in eng}
    acc = {}

    def order(q, reads, writes):
        toks = {}
        for w, specs in ((False, reads), (True, writes)):
            for (n, lo, hi) in specs:
                ps = SCRATCH[n][0] == "psum"
                for (l2, h2, w2, q2, sem, val, kn) in acc.get(n, []):
                    if ps:
                        if q2 == q and (q == "P" or not (w or w2)): continue
                    elif not (w or w2) or lo >= h2 or l2 >= hi:
                        continue
                    if toks.get(sem, (0,))[0] < val: toks[sem] = (val, kn)
        for sem, (val, kn) in sorted(toks.items(), key=lambda t: -sum(t[1][1].values())):
            if know[q].get(sem, 0) < val:
                eng[q].wait_ge(T.sem[sem], val)
                for s2, v2 in list(kn.items()) + [(sem, val)]:
                    if know[q].get(s2, 0) < v2: know[q][s2] = v2

    def note(q, reads, writes, sem, val, kn):
        for w, specs in ((False, reads), (True, writes)):
            for (n, lo, hi) in specs:
                a = acc.setdefault(n, [])
                if SCRATCH[n][0] == "psum":
                    a[:] = [e for e in a if not (e[3] == q and e[2] <= w)]
                else:
                    a[:] = [e for e in a if not (lo <= e[0] and e[1] <= hi and (w or (e[3] == q and e[4] == sem and not e[2])))]
                a.append((lo, hi, w, q, sem, val, kn))

    def op(q, fn, reads, writes):
        order(q, reads, writes)
        fn().then_inc(T.sem["q" + q], 1)
        due["q" + q] += 1
        note(q, reads, writes, "q" + q, due["q" + q], dict(know[q]))

    def dma(q, sem, out, in_, total=16):
        order(q, in_[1], out[1])
        eng[q].dma_start(out[0], in_[0]).then_inc(T.sem[sem], 16)
        due[sem] += 16
        note(q, in_[1], out[1], sem, total, dict(know[q]))

    def b(n, lo=0, hi=None, step=1):
        hi = SCRATCH[n][1][1] if hi is None else hi
        return (T[n][:, lo:hi:step] if step != 1 else T[n][:, lo:hi], [(n, lo, hi)])

    def ext(ap):
        return (ap, [])

    def ind(win, off):
        return (win[0].indirect(off[0]), win[1] + off[1])

    def num(s):
        return (s[0], s[1]) if isinstance(s, tuple) else (s, [])

    def tt(out, in0, in1, o):
        op("V", lambda: g.vector.tensor_tensor(out[0], in0[0], in1[0], o), in0[1] + in1[1] + out[1][1:], out[1][:1])

    def ts(out, in0, s1, s2, o0, o1=None):
        a1, r1 = num(s1)
        a2, r2 = num(s2)
        if o1 is None:
            op("V", lambda: g.vector.tensor_scalar(out[0], in0[0], a1, None, o0), in0[1] + r1, out[1])
        else:
            op("V", lambda: g.vector.tensor_scalar(out[0], in0[0], a1, a2, o0, o1), in0[1] + r1 + r2, out[1])

    def cp(out, in_):
        op("V", lambda: g.vector.tensor_copy(out[0], in_[0]), in_[1] + out[1][1:], out[1][:1])

    def fill(out, c):
        op("V", lambda: g.vector.memset(out[0], c), [], out[1])

    def scan(out, d0, d1, o0, o1):
        op("V", lambda: g.vector.tensor_tensor_scan(out[0], d0[0], d1[0], 0.0, o0, o1), d0[1] + d1[1], out[1])

    def act(out, in_, f=F.Copy, scale=1.0):
        op("S", lambda: g.scalar.activation(out[0], in_[0], f, scale=scale), in_[1], out[1])

    def mm(out, l, r, start=True, stop=True):
        op("P", lambda: g.tensor.matmul(out[0], l[0], r[0], start, stop), l[1] + r[1], out[1])

    def iota(out, pat, base, cm, f=True):
        if f:
            op("G", lambda: g.iota(out[0], pat, base, cm, allow_small_or_imprecise_dtypes=True), [], out[1])
        else:
            op("G", lambda: g.iota(out[0], pat, base, cm), [], out[1])

    for k in range(8):
        dma("SY"[k % 2], "dms", b("mS", 16 * k, 16 * k + 16), ext(T.m[k, :]), 128)
    dma("S", "dmc", b("mc"), ext(T.m[:, :]))
    dma("Y", "dbx", b("bxi"), ext(T.bx[:, :]))
    dma("S", "dim", b("imc"), ext(T.im[:, :]))
    dma("Y", "dbz", b("bzi"), ext(T.bz[:, :]))
    dma("Y", "dz", b("Z", 0, NV), ext(T.z[:, :]))
    dma("Y", "dnz", b("nzt", 0, NV), ext(T.nz[:, :]))
    dma("Y", "dnb", b("nbt", 0, NV), ext(T.nb[:, :]))
    dma("Y", "dx", b("X", 0, NV), ext(T.x[:, :]))

    iota(b("ip32"), [[0, 1]], 0, 1, False)
    iota(b("ipf"), [[0, 1]], 0, 1)
    iota(b("rowI"), [[1, 128]], 0, 0)
    iota(b("rowG"), [[1, 8], [0, 16]], 0, 0)
    iota(b("rowT"), [[0, 16], [1, 16]], 0, 0)
    iota(b("rowc"), [[0, 5], [1, 8]], 0, 0)
    iota(b("l15i"), [[16, 16]], 15, 0, False)
    iota(b("bci"), [[1, 8]], 0, 0, False)
    iota(b("vl"), [[256, 8]], 0, 0)
    iota(b("rowGG"), [[1, 8], [0, 128]], 0, 0)
    for n in ("mrep", "imrep", "nbt", "nzt", "X"):
        iota(b(n, NV, NW), [[0, NW - NV]], 0, 0, n[0] != "n")
    ts(b("If"), b("rowI"), b("ipf"), None, A.is_equal)
    ts(b("pmi"), b("ip32"), 15, None, A.bitwise_and)
    ts(b("pgi"), b("ip32"), 4, None, A.arith_shift_right)
    cp(b("pm"), b("pmi"))
    cp(b("pg"), b("pgi"))
    ts(b("BOh"), b("rowG"), b("pg"), None, A.is_equal)
    ts(b("diag"), b("rowT"), b("pm"), None, A.is_equal)
    cp(b("mSf"), b("mS"))
    mm(b("k0", 0, 128), b("mSf"), b("If"))
    cp(b("ML"), b("k0", 0, 128))
    cp(b("BXL"), b("bxi"))
    cp(b("BZL"), b("bzi"))
    for t in range(16):
        ts(b("LT", 128 * t, 128 * t + 128), b("BOh"), b("diag", t, t + 1), None, A.mult)
    cp(b("mch"), b("mc"))
    cp(b("imch"), b("imc"))
    for t in range(16):
        mm(b("k%d" % (4 + t // 4), t % 4 * 128, t % 4 * 128 + 128), b("LT", 128 * t, 128 * t + 128), b("mch"))
    for t in range(16):
        mm(b("k%d" % (t // 4), t % 4 * 128, t % 4 * 128 + 128), b("LT", 128 * t, 128 * t + 128), b("imch"))
    cp(b("Y", 0, 1024), ind(b("Z", 0, NV), b("ML", 0, 64)))
    act(b("Y", 1024, 2048), ind(b("Z", 0, NV), b("ML", 64, 128)))

    def engines_to(src, dst):
        e = topo.engines(src, dst)
        if topo.chip(src) != topo.chip(dst):
            return e
        far = [c for c in T.cores if topo.chip(c) != topo.chip(src) and topo.may_write(src, c)]
        used = topo.engines(src, far[0])
        return [k for k in e if k not in used]

    def send(rd):
        cp(b("sb%d" % rd, 0, 128), ind(b("Y", 0, NV), b("BXL")))
        act(b("sb%d" % rd, 128, 256), ind(b("Z", 0, NV), b("BZL")))
        groups = {}
        for d in (1, 2, 3):
            dst = T.cores[(rank - d) % N]
            groups.setdefault(tuple(engines_to(core, dst)), []).append((d, dst))
        order("G", b("sb%d" % rd)[1], [])
        tr = []
        for e, ds in groups.items():
            ids = []
            for d, dst in ds:
                rid, pid, _ = topo.addr(dst)
                ids.append(DstId(rid=rid, pnc=pid))
            tr.append(RemoteDMATransfer(dst_ids=ids, dma_engine_mask=sum(1 << k for k in e), remote_sem=T.sem["arr%d" % rd],
                                        srcs=[T["sb%d" % rd][:, :]], dsts=[T["st%d" % rd][:, d - 1, :] for d, _ in ds]))
            due["sent"] += len(e)
        g.remote_dma_fused(tr, local_sem=T.sem["sent"])
        due["arr%d" % rd] = sum(len(engines_to(T.cores[(rank + d) % N], core)) for d in (1, 2, 3))
        note("G", [], [("st%d" % rd, 0, 768)], "arr%d" % rd, due["arr%d" % rd], {})

    send(0)
    ts(b("ind"), b("rowc", 0, 8), b("pg"), None, A.is_equal)
    for k in range(4):
        act(b("mrep", 512 * k, 512 * k + 512), b("k%d" % (4 + k)))
    for k in range(4):
        cp(b("imrep", 512 * k, 512 * k + 512), b("k%d" % k))
    ts(b("segm"), b("rowT"), 0.0, None, A.is_gt)
    ts(b("cK"), b("rowT", 0, 128), -1.0, 15.0, A.mult, A.add)
    act(b("bi16", 0, 8), b("ind"), F.Copy, 16.0)
    act(b("bip", 0, 8), b("ind"))
    act(b("bim", 0, 8), b("ind"), F.Copy, -1.0)
    act(b("ind16"), b("ind"), F.Copy, 0.0625)
    cp(b("L15"), b("l15i"))
    cp(b("bc"), b("bci"))
    act(b("Ih"), b("If"))
    act(b("Ib"), b("If"))
    ts(b("BOg"), b("rowGG"), b("pg"), 0.0625, A.is_equal, A.mult)
    for k in (0, 128):
        ts(b("tri", k, k + 128), b("rowI"), b("ipf"), 4096.0, A.is_le, A.mult)
    ts(b("dc1"), b("ipf"), 2.0, float(NW), A.mult, A.add)
    ts(b("dc2"), b("dc1"), 256.0, None, A.add)
    for k in range(4):
        ts(b("RD", 8 * k, 8 * k + 8), b("rowc", 8 * k, 8 * k + 8), b("pg"), b("dc%d" % (1 + k % 2)), A.is_equal, A.mult)
    cp(b("RD", 32, 40), b("ind"))
    ts(b("pm16"), b("pm"), 16.0, None, A.mult)
    ts(b("vl"), b("vl"), b("pm16"), None, A.add)
    fill(b("ones"), 1.0)
    fill(b("thh"), 0.0)

    def half(n, k):
        return b(n, 128 * k, 128 * k + 128)

    def ch(n, c):
        return b(n, 512 * c, 512 * c + 512)

    def lst(n, c):
        return b(n, 32 * c, 32 * c + 32)

    def every16(n, base=15, cnt=8):
        return b(n, base, base + 16 * cnt - 15, 16)

    Yw, Zw, Xw = b("Y", 0, NW), b("Z", 0, NW), b("X", 0, NW)
    Mw, Iw, NBw, NZw = b("mrep", 0, NW), b("imrep", 0, NW), b("nbt"), b("nzt")

    def names(rd):
        if rd == 0:
            tt(half("WPm", 0), b("mrep", 0, NV, 16), half("diag", 0), A.mult)
            cp(b("nal"), b("nbt", 0, NV, 16))
        else:
            tt(half("WPm", 0), ind(Mw, b("VU")), half("diag", 0), A.mult)
            cp(b("nal"), ind(NBw, b("VU")))
        scan(half("WPs", 0), half("segm", 0), half("WPm", 0), A.mult, A.add)
        cp(b("naf"), b("nal"))
        cp(b("MVL"), every16("WPs"))
        cp(b("nql"), ind(NZw, b("MVL")))
        cp(b("nqf"), b("nql"))

    names(0)
    for rd in range(ROUNDS):
        last = rd == ROUNDS - 1
        cp((T["Y"][:, NV:NW], [("Y", NV, NW)]), (T["st%d" % rd][:, :, 0:128], [("st%d" % rd, 0, 768)]))
        act((T["Z"][:, NV:NW], [("Z", NV, NW)]), (T["st%d" % rd][:, :, 128:256], [("st%d" % rd, 0, 768)]))
        def dsum(c):
            for k in range(16):
                mm((T["k0"][32 * c:32 * c + 32, k:128:16], [("k0", 0, 128)]), b("AD", 512 * c + k, 512 * c + 512, 16), b("bi16", 0, 8))
        act(ch("ZQ", 0), ind(Zw, lst("nql", 0)))
        cp(ch("ZQ", 1), ind(Zw, lst("nql", 1)))
        tt(ch("DF", 0), ind(Yw, lst("nal", 0)), ch("ZQ", 0), A.subtract)
        act(ch("ZQ", 2), ind(Zw, lst("nql", 2)))
        act(ch("AD", 0), ch("DF", 0), F.Abs)
        dsum(0)
        tt(ch("DF", 1), ind(Yw, lst("nal", 1)), ch("ZQ", 1), A.subtract)
        act(ch("ZQ", 3), ind(Zw, lst("nql", 3)))
        act(ch("AD", 1), ch("DF", 1), F.Abs)
        mm(b("k1", 0, 128), b("naf"), b("If"))
        mm(b("k1", 128, 256), b("nqf"), b("If"))
        dsum(1)
        for c in (2, 3):
            tt(ch("DF", c), ind(Yw, lst("nal", c)), ch("ZQ", c), A.subtract)
            act(ch("AD", c), ch("DF", c), F.Abs)
            dsum(c)
        tt(b("KEY"), b("k0", 0, 128), b("cK"), A.add)
        scan(b("MX"), half("segm", 0), b("KEY"), A.mult, A.max)
        tt(b("OH"), ind(b("MX"), b("L15", 0, 8)), b("KEY"), A.is_equal)
        tt(half("PAQ", 0), b("OH"), b("k1", 0, 128), A.mult)
        tt(half("PAQ", 1), b("OH"), b("k1", 128, 256), A.mult)
        scan(b("SC"), b("segm"), b("PAQ"), A.mult, A.add)
        tt(b("E"), ind(b("SC"), b("L15")), b("diag"), A.mult)
        act(b("E2"), ind(b("SC"), b("L15")))
        mm(b("k2", 8, 16), half("E", 1), b("ind"))
        mm(b("k2", 0, 8), half("E", 0), b("ind"))
        cp(b("UL", 16, 24), b("k2", 8, 16))
        cp(b("UL", 0, 8), b("k2", 0, 8))
        cp(b("LBp"), ind(NZw, b("UL", 16, 24)))
        cp(b("LA"), ind(NBw, b("UL", 0, 8)))
        tt(half("WPm", 0), ind(Iw, b("UL", 16, 24)), half("diag", 0), A.mult)
        tt(half("WPm", 1), ind(Mw, b("UL", 0, 8)), half("diag", 1), A.mult)
        scan(b("WPs"), b("segm"), b("WPm"), A.mult, A.add)
        act(ch("Bp", 0), ind(Zw, lst("LBp", 0)))
        cp(b("UL", 8, 16), every16("WPs"))
        cp(b("UL", 24, 32), every16("WPs", 143))
        act(b("LST", 0, 8), b("k2", 0, 8))
        act(b("LST", 16, 24), b("k2", 8, 16))
        for c in (1, 2, 3):
            act(ch("Bp", c), ind(Zw, lst("LBp", c)))
        mm(b("k3", 0, 128), half("E2", 0), b("If"))
        mm(b("k3", 128, 256), half("E2", 1), b("If"))

        def gsum(n, c, sgn, start, stop):
            for k in range(16):
                mm((T["k1"][32 * c:32 * c + 32, 0:8], [("k1", 0, 8)]), b(n, 512 * c + k, 512 * c + 512, 16), b(sgn, 0, 8), start and k == 0, stop and k == 15)

        def gall(n, sgn, start, stop):
            for k in range(16):
                mm(b("k0", 0, 8), b(n, k, 2048, 16), b(sgn, 0, 8), start and k == 0, stop and k == 15)

        def rows(h):
            kb = "k%d" % (2 + h % 2)
            for e in (0, 1):
                gg = 2 * h + e
                mm(b(kb, 256 * e, 256 * e + 256), b("BOg", 128 * gg, 128 * gg + 128), b("RH"), True, False)
                mm(b(kb, 256 * e, 256 * e + 256), b("Ih"), b("tri"), False, True)
            act(ch("RR", h), b(kb))

        def compare(h):
            for gg in (2 * h, 2 * h + 1):
                for s in (0, 1):
                    col = b("SC", 16 * gg + 15, 16 * gg + 16) if s == 0 else b("WS", gg, gg + 1)
                    ts(b("EQ", (2 * gg + s) * 256, (2 * gg + s) * 256 + 256), b("RR", 256 * gg, 256 * gg + 256), col, None, A.is_equal)

        def topb(c):
            mm(b("k%d" % (4 + 2 * (c % 2))), b("Ib"), ch("Bp", c))

        def tops(c):
            mm(b("k%d" % (5 + 2 * (c % 2))), b("Ib"), ch("Bb", c))

        topb(0)
        topb(1)
        for c in range(4):
            tt(ch("M1", c), ind(Yw, lst("LA", c)), ch("Bp", c), A.max)
            if c == 0:
                cp(b("LB"), ind(NZw, b("UL", 24, 32)))
            if c == 1:
                cp(b("LAp"), ind(NBw, b("UL", 8, 16)))
        act(ch("Bb", 0), ind(Zw, lst("LB", 0)))
        act(ch("Bb", 1), ind(Zw, lst("LB", 1)))
        act(half("RP", 1), ind(Iw, b("UL", 16, 24)))
        act(half("RP", 0), b("k3", 0, 128))
        act(b("RH"), b("RP", 0, 256))
        mm(b("k2", 0, 8), half("RP", 1), b("ind16"))
        act(ch("Bb", 2), ind(Zw, lst("LB", 2)))
        act(b("WS"), b("k2", 0, 8))
        act(half("RP", 2), b("k3", 128, 256))
        act(ch("Bb", 3), ind(Zw, lst("LB", 3)))
        act(half("RP", 3), ind(Mw, b("UL", 0, 8)))
        act(b("LST", 8, 16), every16("WPs"))
        act(b("LST", 24, 32), every16("WPs", 143))
        act(b("ZQP"), ind(Zw, b("UL", 16, 32)))
        for c in range(4):
            tt(ch("M2", c), ind(Yw, lst("LA", c)), ch("Bb", c), A.max)
        tops(0)
        tops(1)
        rows(0)
        rows(1)
        gall("M1", "bim", True, False)
        act(ch("Ap", 0), ind(Yw, lst("LAp", 0)))
        act(ch("Ap", 1), ind(Yw, lst("LAp", 1)))
        rows(2)
        rows(3)
        gall("M2", "bip", False, True)
        act(ch("Ap", 2), ind(Yw, lst("LAp", 2)))
        act(ch("Ap", 3), ind(Yw, lst("LAp", 3)))
        ts(b("bad"), every16("MX"), 16.0, None, A.is_lt)
        ts(b("bad2"), every16("SC", 15, 16), float(NV), None, A.is_ge)
        tt(b("bad"), b("bad"), b("bad2", 0, 8), A.add)
        tt(b("bad"), b("bad"), b("bad2", 8, 16), A.add)
        ts(b("thr"), b("bad"), 1.0e6, b("thh"), A.mult, A.add)
        tt(b("XD"), ind(Xw, b("UL", 0, 16)), b("ZQP"), A.subtract)
        compare(0)
        compare(1)
        ts(b("CL"), b("XD"), 1.0, -1.0, A.min, A.max)

        def late(c):
            tt(ch("M3", c), ch("Ap", c), b("k%d" % (4 + 2 * (c % 2))), A.max)
            tt(ch("M4", c), ch("Ap", c), b("k%d" % (5 + 2 * (c % 2))), A.max)
            if c < 2:
                topb(c + 2)
                tops(c + 2)
            gsum("M3", c, "bip", True, False)
            gsum("M4", c, "bim", False, True)

        late(0)
        compare(2)
        late(1)
        compare(3)
        tt(b("thr2"), b("thr"), b("k0", 0, 8), A.subtract)
        late(2)
        late(3)
        tt(b("prop8", 0, 8), b("k1", 0, 8), b("thr2"), A.is_gt)
        for gg in range(8):
            for i in range(4):
                o = (2 * gg + i // 2) * 256 + i % 2 * 128
                mm(b("k2", gg, gg + 1), b("EQ", o, o + 128), b("prop8", gg, gg + 1), i == 0, i == 3)
        if not last:
            ts(b("nvi"), b("vl"), 5.0, 1.0, A.mult, A.add)
            ts(b("nvi"), b("nvi"), 2047, None, A.bitwise_and)
            cp(b("nv5"), b("nvi"))
            ts(b("own"), b("LST", 16, 24), float(NV), None, A.is_lt)
            tt(b("ea"), b("LST", 8, 16), b("nv5"), A.subtract)
            tt(b("ea"), b("ea"), b("own"), A.mult)
            tt(b("ea"), b("ea"), b("nv5"), A.add)
            tt(b("ea"), b("ea"), b("LST", 0, 8), A.subtract)
        tt(b("nc"), b("k2", 0, 8), b("prop8", 0, 8), A.is_ge)
        tt(b("EC"), ind(b("nc"), b("bc")), half("diag", 0), A.mult)
        mm(b("k3", 0, 40), b("EC"), b("RD"))
        tt(b("OF"), b("LST"), b("k3", 0, 32), A.max)

        def scat(n, o):
            return (T[n][:, 0:DUMP].indirect(T["OF"][:, o:o + 16]), [(n, 0, DUMP), ("OF", o, o + 16)])

        tt(scat("Z", 16), b("CL"), b("ZQP"), A.add)
        if last:
            dma("Y", "dzo", ext(T.zo[:, :]), b("Z", 0, NV))
            cp(scat("mrep", 0), b("RP", 256, 512))
            dma("S", "dmo", ext(T.mo[:, :]), (T["mrep"][0:128:16, 0:NV], [("mrep", 0, NV)]))
            break
        tt(scat("Y", 0), b("CL"), b("ZQP"), A.add)
        send(rd + 1)
        tt(b("tv"), b("k3", 32, 40), b("ea"), A.mult)
        tt(b("VU"), b("tv"), b("LST", 0, 8), A.add)
        mm(b("k2", 0, 8), b("ones"), b("nc"))
        cp(scat("mrep", 0), b("RP", 256, 512))
        names(1)
        op("V", lambda: g.vector.tensor_reduce(T["cn"][:, :], T["k2"][:, 0:8], AxisListType.X, A.add), [("k2", 0, 8)], [("cn", 0, 1)])
        ts(b("tha"), b("cn"), -1.0, None, A.mult)
        ts(b("thb"), b("tha"), 31, None, A.bitwise_and)
        ts(b("thh"), b("thb"), 0.5, None, A.mult)
        cp(scat("imrep", 16), b("RP", 0, 256))
    for s in SEMAPHORES:
        if know["G"].get(s, 0) < due[s] and due[s]:
            g.wait_ge(T.sem[s], due[s])
